import numpy as np, ml_dtypes
CORES = [13,21,141,149]
N = 4
BF = ml_dtypes.bfloat16
def gentries(a):
    return np.ascontiguousarray(a.reshape(8, 16, -1).transpose(0, 2, 1)).reshape(8, -1)
def gtable(e):
    e = np.asarray(e); return np.ascontiguousarray(e.reshape(8, -1, 16).transpose(0, 2, 1)).reshape(128, -1).astype(np.int32)
V, E, R, B = 1024, 384, 6, 3
W = N * V
def parts(rng):
    m = np.floor(rng.random((8, 16, W)) * rng.choice(np.array([2, 3, 6, 16]), (8, 1, W))).astype(np.int64)
    ring = rng.integers(0, W, (N, 8, R, V)); u = np.ascontiguousarray(np.argsort(rng.random((N, 8, B, V)), axis=-1)[..., :E])
    return m, ring, u, rng.integers(0, W, (N, 8, B, E))
def pack(m, ring, u, v):
    return {"m0": np.repeat(m.reshape(1, 128, W), N, axis=0).astype(BF), "ring0": np.ascontiguousarray(ring.reshape(N, 8 * R, V)).astype(np.int32),
            "eu": np.stack([gtable(a.reshape(8, -1)) for a in u]), "ev": np.stack([gtable(a.reshape(8, -1)) for a in v])}
def setup_inputs(rng):
    return pack(*parts(rng))
def setup_inputs_ties(rng):
    m, ring, u, v = parts(rng)
    for g in range(8):
        if g % 4 == 0:
            for k in range(R): ring[:, g, k] = ring[:, g, k // 2 * 2]
        if g % 4 == 1: ring[:, g] = ring[:, g, :1]
        if g % 4 == 2: m[g] = rng.integers(0, 16, (16, 3))[:, rng.integers(0, 3, W)]
        if g % 4 == 3: m[g] = rng.integers(0, 2, (16, W)) * rng.integers(0, 2, (1, W))
    return pack(m, ring, u, v)
def setup_inputs_after(rng):
    m, ring, u, v = parts(rng)
    u[:, 4:6] = np.take_along_axis(np.repeat(u[:, 4:6, :1], B, axis=2), np.argsort(rng.random((N, 2, B, E)), axis=-1), axis=-1)
    nodes = u + np.arange(N).reshape(N, 1, 1, 1) * V
    for q in range(N):
        o = (q + int(rng.integers(1, N))) % N
        v[q, ::2, 1:] = nodes[o, ::2, :-1]; v[q, 1::2] = nodes[o, 1::2]
    return pack(m, ring, u, v)
def setup_inputs_alike(rng):
    m, ring, u, v = parts(rng); own = np.arange(N).reshape(N, 1, 1) * V
    v[:, :2] = rng.integers(0, W, (N, 2, B, 1))
    for q in range(N): ring[q, 1] = rng.integers(0, V, (R, V)) + (q + int(rng.integers(1, N))) % N * V
    v[:, 2] = u[:, 2] + own
    ring[:, 3] = np.arange(V) + own
    hot = int(rng.integers(0, W)); ring[:, 4] = hot; m[4, :, hot] = rng.integers(1, 16, 16)
    ring[:, 5] = rng.integers(0, V, (N, R, V)) + own; v[:, 5] = rng.integers(0, V, (N, B, E)) + own
    ring[:, 6] = (rng.integers(V, W, (N, R, V)) + own) % W; v[:, 6] = (rng.integers(V, W, (N, B, E)) + own) % W
    u[:, 7] = np.arange(E); u[:, 7, 1] = np.arange(V - E, V)
    first = int(rng.integers(0, N)) * V; ring[:, 7] = rng.integers(0, V, (N, R, V)) + first; v[:, 7] = rng.integers(0, V, (N, B, E)) + first
    return pack(m, ring, u, v)
def setup_inputs_ends(rng):
    m, ring, u, v = parts(rng)
    m = 15 * (rng.random((8, 16, W)) < rng.choice(np.array([0.1, 0.5, 1.0]), (8, 1, W))).astype(np.int64); m[0] = 15; m[1] = 0
    m[2:4] = rng.integers(12, 15, (2, 16, 1)) + rng.integers(-1, 2, (2, 16, W)) * (rng.random((2, 16, W)) < np.array([1.0, 0.125]).reshape(2, 1, 1))
    mid = np.argsort(rng.random((N, 8, B, V - 2)), axis=-1)[..., :E - 2] + 1
    u = np.concatenate([np.full((N, 8, B, 1), V - 1), mid, np.zeros((N, 8, B, 1), np.int64)], axis=3)
    ends = np.concatenate([np.arange(N) * V, np.arange(N) * V + V - 1])
    ring[:, 5:] = rng.choice(ends, (N, 3, R, V)); v[:, 5:] = rng.choice(ends, (N, 3, B, E))
    return pack(m, ring, u, v)
def setup_inputs_spread(rng):
    m, ring, u, v = parts(rng)
    m = np.floor(16 * rng.random((8, 16, W)) * np.exp2(-rng.integers(0, 5, (8, 1, W)))).astype(np.int64)
    o = np.argsort(rng.random((8, W)), axis=-1)
    for g in range(8):
        ring[:, g] = o[g][np.minimum((W * rng.random((N, R, V)) ** 4).astype(np.int64), W - 1)]
        v[:, g] = o[g][np.minimum((W * rng.random((N, B, E)) ** 4).astype(np.int64), W - 1)]
    u = np.ascontiguousarray(np.argsort(rng.random((N, 8, B, V)) * np.exp2(3 * rng.random((N, 8, 1, V))), axis=-1)[..., :E])
    return pack(m, ring, u, v)
def check_inputs(d):
    bad = []; a = np.asarray(d["m0"]).astype(np.float32)
    if not np.all((a >= 0) & (a <= 15) & (a == np.floor(a))): bad.append("range of m0")
    if not np.all(a == a[:1]): bad.append("m0 alike on all ranks")
    for k, hi in (("ring0", W - 1), ("eu", V - 1), ("ev", W - 1)):
        if np.min(d[k]) < 0 or np.max(d[k]) > hi: bad.append("range of " + k)
    s = np.sort(np.stack([gentries(x) for x in d["eu"]]).reshape(N, 8, B, E), axis=-1)
    if np.any(s[..., 1:] == s[..., :-1]): bad.append("u distinct in a batch")
    return bad
def reference(m0, ring0, eu, ev):
    m = m0[0].astype(np.int64).reshape(8, 16, W); ring = ring0.astype(np.int64).reshape(N, 8, R, V).copy(); gi = np.arange(8)[:, None]
    us = np.stack([gentries(a) for a in eu]).astype(np.int64).reshape(N, 8, B, E); vs = np.stack([gentries(a) for a in ev]).astype(np.int64).reshape(N, 8, B, E)
    for b in range(B):
        new = m.copy()
        for q in range(N):
            u, v = us[q, :, b], vs[q, :, b]
            ids = np.take_along_axis(ring[q], np.broadcast_to(u[:, None, :], (8, R, E)), 2)
            mi = np.take_along_axis(m, ids.reshape(8, 1, R * E), 2).reshape(8, 16, R, E)
            mu = np.take_along_axis(m, u[:, None, :] + q * V, 2); mv = np.take_along_axis(m, v[:, None, :], 2)
            c = np.sum(mi * mv[:, :, None, :], axis=1)
            k = np.argmin(c, axis=1)
            np.put_along_axis(new, np.broadcast_to(u[:, None, :] + q * V, (8, 16, E)), np.clip(mu + mv - np.max(mi, axis=2), 0, 15), 2)
            ring[q][gi, k, u] = v
        m = new
    full = m.reshape(128, W)
    return {"ym": np.stack([full[:, q * V:(q + 1) * V] for q in range(N)]).astype(BF), "yr": ring.reshape(N, 8 * R, V).astype(np.float32)}

from concourse.bass import DstId, RemoteDMATransfer
from concourse.mybir import AluOpType, ActivationFunctionType

V, E, R, B, N = 1024, 384, 6, 3, 4
W = N * V
C16 = E // 16
CUT = 256

SCRATCH = {
    "w0": ("sbuf", [128, W], "bfloat16"), "w1": ("sbuf", [128, W], "bfloat16"), "w2": ("sbuf", [128, W], "bfloat16"),
    "land": ("sbuf", [128, (B - 1) * V], "bfloat16"),
    "ringi": ("sbuf", [128, V], "int32"), "ringf": ("sbuf", [128, V], "float32"),
    "eui": ("sbuf", [128, B * C16], "int32"), "evi": ("sbuf", [128, B * C16], "int32"),
    "uo": ("sbuf", [128, B * C16], "uint16"), "vo": ("sbuf", [128, B * C16], "uint16"), "ur": ("sbuf", [128, B * C16], "uint16"),
    "evf": ("sbuf", [128, B * C16], "float32"), "vdiag": ("sbuf", [128, B * E], "float32"),
    "g16": ("sbuf", [128, E], "float16"), "tt": ("sbuf", [128, E], "float32"),
    "offs": ("sbuf", [128, B * R * C16], "uint16"),
    "mi": ("sbuf", [128, R * E], "bfloat16"), "prod": ("sbuf", [128, R * E], "bfloat16"),
    "mv": ("sbuf", [128, E], "bfloat16"), "mu": ("sbuf", [128, E], "bfloat16"),
    "r1": ("sbuf", [128, E], "bfloat16"), "r2": ("sbuf", [128, E], "bfloat16"), "mx": ("sbuf", [128, E], "bfloat16"),
    "tn": ("sbuf", [128, E], "bfloat16"), "newv": ("sbuf", [128, E], "bfloat16"),
    "sg": ("sbuf", [128, E], "bfloat16"), "mark": ("sbuf", [128, E], "float32"),
    "negold": ("sbuf", [128, E], "float32"), "td": ("sbuf", [128, E], "float32"),
    "ia": ("sbuf", [128, 16], "int32"), "ib": ("sbuf", [128, 8], "int32"),
    "ia2": ("sbuf", [128, 16], "int32"), "ib2": ("sbuf", [128, 8], "int32"),
    "m16": ("sbuf", [128, 16], "float32"), "gm": ("sbuf", [128, 8], "float32"),
    "ones": ("sbuf", [128, 128], "bfloat16"), "ones32": ("sbuf", [128, 128], "float32"),
    "swp": ("sbuf", [128, 4 * 128], "bfloat16"), "idb": ("sbuf", [128, 128], "bfloat16"), "nid": ("sbuf", [128, 128], "bfloat16"),
    "id32": ("sbuf", [128, 128], "float32"), "bd": ("sbuf", [128, 128], "float32"),
    "cf": ("sbuf", [128, R * 16], "bfloat16"), "lm": ("sbuf", [128, R, 8, 16], "bfloat16"),
    "wm": ("sbuf", [128, 8, 16], "bfloat16"),
    "pp": ("psum", [128, 512], "float32"), "ps": ("psum", [128, 512], "float32"), "pv": ("psum", [128, 512], "float32"),
    "pd": ("psum", [128, 512], "float32"), "px": ("psum", [128, 16, 2, 16], "float32"),
    "pa": ("psum", [128, 512], "float32"), "pb": ("psum", [128, 512], "float32"), "pw": ("psum", [128, 512], "float32"),
}
SEMAPHORES = (["ldl", "ldr", "ldma", "ldmb", "ldw1", "st", "sent", "hin0", "hin1", "arr0", "arr1",
               "zr", "iab", "iab2", "m16", "gm", "cz", "cf", "lm", "wz", "uo", "ur", "urr", "vo", "evf", "vd", "one", "one32", "swp",
               "idb", "nid", "id32", "bd1", "bd", "wmm", "wm", "conv", "cpy",
               "mv", "r1", "r2", "p1", "p2", "p3", "p4", "mx", "tn", "newv", "ms", "s", "pv", "pm", "df",
               "d0", "d1", "sg0", "sg1", "wn0", "wn1", "mk0", "mk1", "td", "rs", "no", "mu", "rg", "x", "tt", "cv0", "cvr"]
              + ["mi%d" % k for k in range(R)] + ["pr%d_%d" % (h, k) for h in range(2) for k in range(R)])

A = AluOpType
F = ActivationFunctionType


def split(lst, n):
    k = len(lst) // n
    return [sum(1 << e for e in lst[i * k:(i + 1) * k]) for i in range(n)]


def ones_in(m):
    return bin(m).count("1")


def routes(c, T, topo):
    others = [d for d in T.cores if d != c]
    near = [d for d in others if topo.may_write(c, d)]
    far = [d for d in others if d not in near]
    helpers = [h for h in topo.cores_of(c) if T.rank_of(h) is None and far and all(topo.may_write(h, d) for d in far)]
    return near, far, helpers


def helper_masks(h, far, topo):
    return split(topo.engines(h, far[0]), len(far))


def arrivals(c, T, topo):
    n = 0
    for s in T.cores:
        if s == c:
            continue
        near, far, helpers = routes(s, T, topo)
        if c in near:
            n += ones_in(split(topo.engines(s, c), len(near))[near.index(c)])
        else:
            n += sum(ones_in(helper_masks(h, far, topo)[far.index(c)]) for h in helpers)
    return n


def dst(d, src, topo):
    rid, pid = topo.addr(d, src)
    return DstId(rid=rid, pnc=pid)


def helper_program(g, core, owner, T, topo):
    near, far, helpers = routes(owner, T, topo)
    i = helpers.index(core)
    q = V // len(helpers)
    got = ones_in(split(topo.engines(owner, core), len(helpers))[i])
    masks = helper_masks(core, far, topo)
    o = T.rank_of(owner) * V + i * q
    total = 0
    for b in range(B - 1):
        g.wait_ge(T.sem["hin%d" % b], got)
        g.remote_dma_fused([RemoteDMATransfer(dst_ids=[dst(d, core, topo)], dma_engine_mask=m, remote_sem=T.sem["arr%d" % b],
                                              src=T.land[:, b * V:b * V + q], dst=T["w%d" % (b + 1)][:, o:o + q])
                            for d, m in zip(far, masks)], local_sem=T.sem.sent)
        total += sum(ones_in(m) for m in masks)
    g.wait_ge(T.sem.sent, total)


def rank_program(g, core, T, topo):
    rank = T.rank_of(core)
    if rank is None:
        for owner in T.cores:
            if core in routes(owner, T, topo)[2]:
                helper_program(g, core, owner, T, topo)
        return

    prog = {"g": [], "pe": [], "dve": [], "act": [], "sp": []}
    eng = {"g": g, "pe": g.tensor, "dve": g.vector, "act": g.scalar, "sp": g.sync}
    added = {}

    def op(q, fn, after=(), inc=None, n=1):
        prog[q].append((fn, list(after), inc, n))
        if inc is not None:
            added[inc] = added.get(inc, 0) + n

    S = -1
    own = slice(rank * V, (rank + 1) * V)
    win = [T.w0, T.w1, T.w2]
    vec, act, pe = g.vector, g.scalar, g.tensor
    near, far, helpers = routes(core, T, topo)
    for b in range(B - 1):
        added[("arr%d" % b, S)] = arrivals(core, T, topo)

    def ul(b):
        return T.uo[:, b * C16:(b + 1) * C16]

    def ol(b, k):
        return T.offs[:, (b * R + k) * C16:(b * R + k + 1) * C16]

    def mi(k, a=0, z=E):
        return T.mi[:, k * E + a:k * E + z]

    def pr(k, a, z):
        return T.prod[:, k * E + a:k * E + z]

    half = W // 2
    ha = slice(0, half) if rank * V < half else slice(half, W)
    hb = slice(half, W) if rank * V < half else slice(0, half)
    op("sp", lambda: g.sync.dma_start(T.eui[:], T.eu[:]), inc=("ldl", S), n=16)
    op("sp", lambda: g.sync.dma_start(T.evi[:], T.ev[:]), inc=("ldl", S), n=16)
    op("act", lambda: act.dma_start(T.w0[:, ha], T.m0[:, ha]), inc=("ldma", S), n=16)
    op("dve", lambda: vec.memset(T.ringi[:], 0), inc=("zr", S))
    for k in range(R):
        q = "sp" if k % 2 == 0 else "act"
        op(q, lambda k=k, q=q: eng[q].dma_start(T.ringi[k::16, :], T.ring0[k::R, :]), after=[("zr", S)], inc=("ldr", S), n=16)
    op("sp", lambda: g.sync.dma_start(T.w0[:, hb], T.m0[:, hb]), inc=("ldmb", S), n=16)
    op("sp", lambda: g.sync.dma_start(T.w1[:, own], T.m0[:, own]), after=[("ldmb", S)], inc=("ldw1", S), n=16)

    op("g", lambda: g.iota(T.ia[:], [[-1, 16]], 128, 1), inc=("iab", S))
    op("g", lambda: g.iota(T.ib[:], [[-16, 8]], 128, 1), inc=("iab", S))
    op("g", lambda: g.iota(T.ones[:], [[0, 128]], 1, 0, allow_small_or_imprecise_dtypes=True), inc=("one", S))
    for s in range(2):
        for h in range(2):
            j = 2 * s + h
            op("g", lambda s=s, h=h, j=j: g.affine_select(T.swp[:, j * 128:(j + 1) * 128], T.ones[:], [[-32, 4], [1000, 2], [-1, 16]],
                                                          A.is_equal, 0.0, -16 * s - 1000 * h, 1),
               after=[("one", S)], inc=("swp", S))
    op("g", lambda: g.affine_select(T.idb[:], T.ones[:], [[-1, 128]], A.is_equal, 0.0, 0, 1), inc=("idb", S))
    op("g", lambda: g.iota(T.ones32[:], [[0, 128]], 1, 0, allow_small_or_imprecise_dtypes=True), inc=("one32", S))
    op("g", lambda: g.affine_select(T.bd[:], T.ones32[:], [[-16, 8], [0, 16]], A.is_ge, 0.0, 0, 1), after=[("one32", S)], inc=("bd1", S))
    op("g", lambda: g.affine_select(T.id32[:], T.ones32[:], [[-1, 128]], A.is_equal, 0.0, 0, 1), inc=("id32", S))
    op("g", lambda: g.affine_select(T.bd[:], T.bd[:], [[16, 8], [0, 16]], A.is_ge, 0.0, 15, -1), after=[("bd1", S)], inc=("bd", S))

    op("dve", lambda: vec.memset(T.cf[:], 0.0), inc=("cz", S))
    op("dve", lambda: vec.memset(T.wm[:], 0.0), inc=("wz", S))
    op("dve", lambda: vec.tensor_scalar(T.ia2[:], T.ia[:], 15, None, A.bitwise_and), after=[("iab", S)], inc=("iab2", S))
    op("dve", lambda: vec.tensor_scalar(T.ib2[:], T.ib[:], 4, None, A.arith_shift_right), inc=("iab2", S))
    q0 = 0
    for a in range(R - 1):
        n = R - 1 - a
        op("dve", lambda a=a, n=n, q0=q0: vec.memset(T.cf[:, a * 16 + q0:a * 16 + q0 + n], -1.0), after=[("cz", S)], inc=("cf", S))
        f = (a + 1) * 16 + q0
        op("dve", lambda n=n, f=f: vec.memset(T.cf[:, f:f + 17 * (n - 1) + 1:17], 1.0), inc=("cf", S))
        q0 += n
    op("dve", lambda: vec.tensor_scalar(T.m16[:], T.ia2[:], 0.0, None, A.is_equal), after=[("iab2", S)], inc=("m16", S))
    op("dve", lambda: vec.tensor_scalar(T.gm[:], T.ib2[:], 8.0, None, A.is_equal), inc=("gm", S))
    hc = C16 // 2

    def ring_list(b):
        for h in range(2):
            op("dve", lambda h=h: vec.tensor_copy(T.ur[:, b * C16 + h * hc:b * C16 + (h + 1) * hc], T.eui[:, b * C16 + h:(b + 1) * C16:2]),
               inc=("ur" if b == 0 else "urr", S))

    op("dve", lambda: vec.tensor_copy(T.evf[:], T.evi[:]), after=[("ldl", S)], inc=("evf", S))
    ring_list(0)
    op("dve", lambda: vec.tensor_copy(T.uo[:], T.eui[:]), inc=("uo", S))
    op("dve", lambda: vec.tensor_copy(T.vo[:], T.evi[:]), inc=("vo", S))
    for b in range(1, B):
        ring_list(b)

    def pair_matrices():
        for gi in range(8):
            op("dve", lambda gi=gi: vec.tensor_scalar(T.lm[:, :, gi, :], T.cf[:], T.gm[:, gi:gi + 1], None, A.mult),
               after=[("cf", S), ("gm", S)], inc=("lm", S))

    def vdiag(ps):
        for p in ps:
            op("act", lambda p=p: act.activation(T.vdiag[:, p::16], T.evf[:], F.Copy, scale=T.m16[:, p:p + 1]),
               after=[("evf", S), ("m16", S)], inc=("vd", S))

    vdiag(range(10))
    op("act", lambda: act.activation(T.mu[:], T.w0[:, own].indirect(ul(0)), F.Copy), after=[("ldma", S), ("uo", S)], inc=("mu", 0))

    def lists(b):
        src = T.ringi if b == 0 else T.ringf
        op("dve", lambda: vec.tensor_scalar(T.g16[:], src[:].indirect(T.ur[:, b * C16:(b + 1) * C16]), -2048.0, None, A.add),
           after=[("ldr", S), ("ur", S)] if b == 0 else [("rs", b - 1), ("urr", S)], inc=("rg", b))
        if b == 0:
            pair_matrices()
        for s in range(2):
            for h in range(2):
                j = 2 * s + h
                op("pe", lambda s=s, h=h, j=j: pe.matmul(T.px[:, 0:hc, s, :], T.swp[:, j * 128:(j + 1) * 128],
                                                         T.g16[:, h * E // 2:(h + 1) * E // 2], h == 0, h == 1),
                   after=[("rg", b), ("swp", S)], inc=("x", b) if h == 1 else None)
        op("dve", lambda: vec.transpose(T.tt[:], T.px[:, 0:hc]), after=[("x", b)], inc=("tt", b))
        for k in range(R):
            op("dve", lambda k=k: vec.tensor_scalar(ol(b, k), T.tt[:, k::16], 2048.0, None, A.add), after=[("tt", b)],
               inc=("cv0" if k == 0 else "cvr", b))

    def negold(b):
        op("act", lambda: act.activation(T.negold[:], T.ringf[:].indirect(ul(b)), F.Copy, scale=-1.0),
           after=[("conv", S)] if b == 0 else [("rs", b - 1)], inc=("no", b))

    def diff_old(b):
        op("pe", lambda: pe.matmul(T.pd[:, 0:E], T.id32[:], T.negold[:], False, True), after=[("no", b), ("id32", S)], inc=("df", b))

    def batch(b):
        last = b == B - 1
        w = win[b]
        nxt = win[b] if last else win[b + 1]
        here = [("ldma", S), ("ldmb", S)] if b == 0 else [("arr%d" % (b - 1), S)]
        order = [0, 1, 2, 3, 4, 5] if last else [0, 1, 2, 3, 5, 4]
        parts = [(0, E)] if last else [(0, CUT), (CUT, E)]
        dbank, wbank = [T.pa, T.pb], [T.pw, T.pp]

        for k in order:
            op("act", lambda k=k: act.activation(mi(k), w[:].indirect(ol(b, k)), F.Copy),
               after=here + [("cv0" if k == 0 else "cvr", b)], inc=("mi%d" % k, b))

        def pe_s():
            op("pe", lambda: pe.matmul(T.ps[:, 0:E], T.idb[:], T.mu[:], True, False), after=[("mu", b), ("idb", S)])
            op("pe", lambda: pe.matmul(T.ps[:, 0:E], T.idb[:], T.mv[:], False, not last), after=[("mv", b)], inc=None if last else ("s", b))

        def pe_v():
            op("pe", lambda: pe.matmul(T.pv[:, 0:E], T.idb[:], T.mv[:], True, True), after=[("mv", b), ("idb", S)], inc=("pv", b))

        def pe_m():
            op("pe", lambda: pe.matmul(T.pp[:, 0:E], T.idb[:], mi(1), True, True), after=[("mi1", b)], inc=("pm", b))

        for f in ([pe_v, pe_m, pe_s] if last else [pe_s, pe_m, pe_v]):
            f()
        if b == 0:
            for k in range(R):
                op("pe", lambda k=k: pe.matmul(T.pw[:, k:8 * R:R], T.lm[:, k], T.idb[:, k::16], True, True), after=[("lm", S)], inc=("wmm", S))
            vdiag(range(10, 16))
            op("act", lambda: act.activation(T.wm[:, :, 0:R], T.pw[:, 0:8 * R], F.Copy), after=[("wmm", S), ("wz", S)], inc=("wm", S))
            op("act", lambda: act.activation(T.nid[:], T.idb[:], F.Copy, scale=-1.0), after=[("idb", S)], inc=("nid", S))
        op("pe", lambda: pe.matmul(T.pd[:, 0:E], T.bd[:], T.vdiag[:, b * E:(b + 1) * E], True, False), after=[("vd", S), ("bd", S)])
        if b > 0:
            diff_old(b)

        def product(h, k):
            a, z = parts[h]
            op("dve", lambda: vec.tensor_tensor(pr(k, a, z), mi(k, a, z), T.pv[:, a:z], A.mult),
               after=[("mi%d" % k, b), ("pv", b)], inc=("pr%d_%d" % (h, k), b))

        def differences(h, i):
            a, z = parts[h]
            k = order[i]
            op("pe", lambda: pe.matmul(dbank[h][:, 0:z - a], T.lm[:, k], pr(k, a, z), i == 0, i == R - 1),
               after=[("pr%d_%d" % (h, k), b), ("lm", S)], inc=("d%d" % h, b) if i == R - 1 else None)

        def wins(h):
            a, z = parts[h]
            op("pe", lambda: pe.matmul(wbank[h][:, 0:z - a], T.wm[:], T.sg[:, a:z], True, True), after=[("sg%d" % h, b), ("wm", S)], inc=("wn%d" % h, b))

        op("dve", lambda: vec.tensor_copy(T.mv[:], w[:].indirect(T.vo[:, b * C16:(b + 1) * C16])), after=here + [("vo", S)], inc=("mv", b))
        pp = T.pp[:, 0:E]
        if not last:
            op("dve", lambda: vec.tensor_tensor(T.r1[:], w[:].indirect(ol(b, 5)), mi(0), A.max), after=[("cvr", b), ("mi0", b)], inc=("r1", b))
            op("dve", lambda: vec.tensor_tensor(T.r2[:], w[:].indirect(ol(b, 4)), T.r1[:], A.max), after=[("r1", b)], inc=("r2", b))
            op("dve", lambda: vec.tensor_tensor(pp, T.r2[:], pp, A.max), after=[("r2", b), ("pm", b)], inc=("p1", b))
            op("dve", lambda: vec.tensor_tensor(pp, mi(2), pp, A.max), after=[("p1", b), ("mi2", b)], inc=("p2", b))
            op("dve", lambda: vec.tensor_tensor(T.mx[:], mi(3), pp, A.max), after=[("p2", b), ("mi3", b)], inc=("mx", b))
            op("dve", lambda: vec.tensor_tensor(T.tn[:], T.ps[:, 0:E], T.mx[:], A.subtract), after=[("mx", b), ("s", b)], inc=("tn", b))
            op("dve", lambda: vec.tensor_scalar(T.newv[:], T.tn[:], 0.0, 15.0, A.max, A.min), after=[("tn", b)], inc=("newv", b))
        else:
            def largest(k):
                op("dve", lambda: vec.tensor_tensor(pp if k < R - 1 else T.mx[:], mi(k if k > 1 else 0), pp, A.max),
                   after=[("p%d" % (k - 1), b), ("mi%d" % k, b)] if k > 1 else [("pm", b), ("mi0", b)],
                   inc=("p%d" % k if k < R - 1 else "mx", b))

            product(0, 0)
            largest(1)
            product(0, 1)
            largest(2)
            product(0, 2)
            for k in range(3, R):
                largest(k)
            for k in range(3, R):
                product(0, k)
            for i in range(3):
                differences(0, i)
            op("pe", lambda: pe.matmul(T.ps[:, 0:E], T.nid[:], T.mx[:], False, True), after=[("mx", b), ("nid", S)], inc=("s", b))
            for i in range(3, R):
                differences(0, i)
            wins(0)
            op("act", lambda: act.activation(T.tn[:], T.ps[:, 0:E], F.Relu, bias=15.0, scale=-1.0), after=[("s", b)], inc=("tn", b))
            op("act", lambda: act.activation(T.newv[:], T.tn[:], F.Relu, bias=15.0, scale=-1.0), after=[("tn", b)], inc=("newv", b))
        op("dve", lambda: vec.tensor_copy(nxt[:, own].indirect(ul(b)), T.newv[:]),
           after=[("newv", b), [("ldw1", S), ("cpy", S), ("sent", S)][b]], inc=("ms", b))

        if last:
            op("sp", lambda: g.sync.dma_start(T.ym[:], nxt[:, own]), after=[("ms", b)], inc=("st", S), n=16)
        else:
            q = V // len(helpers)
            hm = split(topo.engines(core, helpers[0]), len(helpers))
            nm = split(topo.engines(core, near[0]), len(near))
            op("g", lambda: g.remote_dma_fused(
                [RemoteDMATransfer(dst_ids=[dst(h, core, topo)], dma_engine_mask=m, remote_sem=T.sem["hin%d" % b],
                                   src=nxt[:, rank * V + i * q:rank * V + (i + 1) * q], dst=T.land[:, b * V:b * V + q])
                 for i, (h, m) in enumerate(zip(helpers, hm))], local_sem=T.sem.sent), after=[("ms", b)])
            op("g", lambda: g.remote_dma_fused(
                [RemoteDMATransfer(dst_ids=[dst(d, core, topo)], dma_engine_mask=m, remote_sem=T.sem["arr%d" % b],
                                   src=nxt[:, own], dst=nxt[:, own]) for d, m in zip(near, nm)], local_sem=T.sem.sent))
            added[("sent", S)] = added.get(("sent", S), 0) + sum(ones_in(m) for m in hm + nm)
            if b == 0:
                op("dve", lambda: vec.tensor_copy(T.ringf[:], T.ringi[:]), inc=("conv", S))
                op("act", lambda: act.activation(T.w2[:, own], T.w1[:, own], F.Copy), after=[("ms", b)], inc=("cpy", S))
                negold(0)
            op("act", lambda: act.activation(T.mu[:], nxt[:, own].indirect(ul(b + 1)), F.Copy), after=[("ms", b)], inc=("mu", b + 1))
            for h in range(len(parts)):
                for k in order:
                    product(h, k)
            for h in range(len(parts)):
                for i in range(R):
                    differences(h, i)
                    if b == 0 and h == 0 and i == 2:
                        diff_old(0)
                    if h == 1 and i == 2:
                        wins(0)
            wins(1)

        for h, (a, z) in enumerate(parts):
            op("act", lambda h=h, a=a, z=z: act.activation(T.sg[:, a:z], dbank[h][:, 0:z - a], F.Sign, bias=0.5), after=[("d%d" % h, b)], inc=("sg%d" % h, b))
            op("act", lambda h=h, a=a, z=z: act.activation(T.mark[:, a:z], wbank[h][:, 0:z - a], F.Relu, bias=-4.0, scale=-1.0),
               after=[("wn%d" % h, b)], inc=("mk%d" % h, b))
            op("dve", lambda h=h, a=a, z=z: vec.tensor_tensor(T.td[:, a:z], T.mark[:, a:z], T.pd[:, a:z], A.mult),
               after=[("mk%d" % h, b), ("df", b)], inc=("td", b))
        op("dve", lambda: vec.tensor_tensor(T.ringf[:].indirect(ul(b)), T.td[:], T.negold[:], A.subtract), after=[("td", b)], inc=("rs", b))
        if last:
            for k in range(R):
                q = "sp" if k % 2 == 0 else "act"
                op(q, lambda k=k, q=q: eng[q].dma_start(T.yr[k::R, :], T.ringf[k::16, :]), after=[("rs", b)], inc=("st", S), n=16)
        else:
            negold(b + 1)
            lists(b + 1)

    lists(0)
    for b in range(B):
        batch(b)

    def upto(key):
        return sum(n for (name, t), n in added.items() if name == key[0] and t <= key[1])

    top = {}
    for q in prog:
        seen = {}
        for fn, after, inc, n in prog[q]:
            for key in after:
                v = upto(key)
                if seen.get(key[0], 0) < v:
                    eng[q].wait_ge(T.sem[key[0]], v)
                    seen[key[0]] = v
                    top[key[0]] = max(top.get(key[0], 0), v)
            ins = fn()
            if inc is not None:
                ins.then_inc(T.sem[inc[0]], n)
    for name in sorted(set(k[0] for k in added)):
        v = upto((name, B))
        if top.get(name, 0) < v:
            (g if name == "sent" else g.sync).wait_ge(T.sem[name], v)
